import numpy as np
import ml_dtypes


def mxq(x, axis, fmt="e4m3"):
    dtype, down = {"e4m3": (ml_dtypes.float8_e4m3fn, 7), "e5m2": (ml_dtypes.float8_e5m2, 14)}[fmt]
    v = np.moveaxis(np.asarray(x, np.float32).astype(ml_dtypes.bfloat16).astype(np.float64), axis, -1)
    blocks = v.reshape(v.shape[:-1] + (-1, 32))
    amax = np.abs(blocks).max(-1, keepdims=True)
    byte = np.maximum(np.where(amax > 0, np.frexp(amax)[1] - 1 + 127, 0) - down, 1)
    scale = np.exp2(byte - 127.0)
    codes = (blocks / scale).astype(np.float32).astype(dtype).astype(np.float64)
    return np.moveaxis((codes * scale).reshape(v.shape), -1, axis)


WIDE = False


def mx_kscale(k):
    if not WIDE:
        return np.ones(k)
    levels = np.array([10, -10, 5, -5, 0])
    if k % 512:
        return np.exp2(np.random.permutation(np.resize(levels, k // 32))).repeat(32)
    a = np.empty((k // 512, 16))
    for p in range(k // 512):
        a[p, :8] = np.random.permutation(np.resize(levels, 8))
        for g in range(8):
            far = levels[np.abs(levels - a[p, g]) >= 10]
            a[p, g + 8] = far[np.random.randint(len(far))]
    return np.exp2(a.ravel()).repeat(32)


def f64(x):
    return np.asarray(x).astype(np.float64)


def striped(idx):
    return np.tile(np.asarray(idx).reshape(-1, 16).T, (8, 1)).astype(np.uint16)


def unstriped(offs):
    return offs[:16].T.reshape(-1).astype(np.int64)


E2M1 = np.array([0.0, 0.5, 1.0, 1.5, 2.0, 3.0, 4.0, 6.0, -0.0, -0.5, -1.0, -1.5, -2.0, -3.0, -4.0, -6.0])


def pack_weight(w, fmt):
    k, n = w.shape
    w = f64(np.asarray(w, np.float32).astype(ml_dtypes.bfloat16)).reshape(k // 32, 32, n)
    amax = np.abs(w).max(1)
    if fmt == "e4m3":
        byte = np.frexp(amax)[1] - 1 + 127 - 7
    else:
        mant, ex = np.frexp(amax / 6.0)
        byte = np.where(mant > 0.5, ex, ex - 1) + 127
    byte = np.clip(np.where(amax > 0, byte, 1), 1, 254)
    scaled = (w * np.exp2(127.0 - byte)[:, None, :]).reshape(k, n).astype(np.float32)
    by_word = np.ascontiguousarray(scaled.reshape(k // 512, 128, 4, n).transpose(0, 1, 3, 2))
    if fmt == "e4m3":
        words = by_word.astype(ml_dtypes.float8_e4m3fn).view(np.uint8)
    else:
        c = by_word.astype(ml_dtypes.float4_e2m1fn).view(np.uint8) & 0xF
        words = (c[..., 0::2] | (c[..., 1::2] << 4)).reshape(k // 512, 128, 2 * n)
    return np.ascontiguousarray(words), np.ascontiguousarray(byte.astype(np.uint8).reshape(k // 512, 16, n))


def unpack_weight(words, scales, fmt):
    g, _, n = scales.shape
    words = np.ascontiguousarray(words).reshape(g, 128, n, -1)
    if fmt == "e4m3":
        vals = words.view(ml_dtypes.float8_e4m3fn).astype(np.float64)
    else:
        nib = np.empty((g, 128, n, 4), np.uint8)
        nib[..., 0::2] = words & 0xF
        nib[..., 1::2] = words >> 4
        vals = E2M1[nib]
    vals = vals * np.repeat(np.exp2(scales.astype(np.float64) - 127.0), 8, axis=1)[..., None]
    return vals.transpose(0, 1, 3, 2).reshape(g * 512, n)


def sigmoid(v):
    return 1.0 / (1.0 + np.exp(-v))


D, T, I, Q, E, M = 512, 1024, 512, 512, 512, 1024


def setup_inputs():
    n = np.random.standard_normal
    idx = np.random.permutation(T)[:I]
    idx2 = np.random.permutation(T)[:I]
    idx3 = np.random.permutation(M)[:I]
    fd = mx_kscale(D)
    fq = mx_kscale(Q)
    keysp = pack_weight(n((D, T)) / fd[:, None], "e4m3")
    return {
        "query": (n((D, Q)) * 1.0 / np.sqrt(D) * fd[:, None]).astype(np.float32),
        "keys_words": keysp[0],
        "keys_scales": keysp[1],
        "qs": (np.random.uniform(0.5, 2.0, (Q, 1)) * fq[:, None]).astype(np.float32),
        "msgs": (n((Q, E)) * 1 / np.sqrt(Q) / fq[:, None]).astype(np.float32),
        "old": (n((E, M)) * 1.0).astype(np.float32),
        "fade": (np.random.uniform(0.3, 0.9, (1, M))).astype(np.float32),
        "offs": striped(idx),
        "offs2": striped(idx2),
        "offs3": striped(idx3),
    }


def reference(query, keys_words, keys_scales, qs, msgs, old, fade, offs, offs2, offs3):
    idx = unstriped(offs)
    idx2 = unstriped(offs2)
    idx3 = unstriped(offs3)
    keysu = unpack_weight(keys_words, keys_scales, "e4m3")
    queryq = mxq(f64(query), 0, "e4m3")
    a = queryq.T @ keysu
    s = a[:, idx] - a[:, idx2]
    w = sigmoid(s)
    wq = w * f64(qs)
    msgsq = mxq(f64(msgs), 0, "e4m3")
    wqq = mxq(wq, 0, "e4m3")
    dl = msgsq.T @ wqq
    df = np.zeros((E, M))
    df[:, idx3] = dl
    y = f64(old) * f64(fade) + df
    return y

@@ -1,0 +1,221 @@
+from contextlib import ExitStack
+
+import concourse.mybir as mybir
+from concourse.masks import make_identity
+
+F32 = mybir.dt.float32
+BF16 = mybir.dt.bfloat16
+I32 = mybir.dt.int32
+U32 = mybir.dt.uint32
+U16 = mybir.dt.uint16
+U8 = mybir.dt.uint8
+FP8X4 = mybir.dt.float8_e4m3fn_x4
+ACT = mybir.ActivationFunctionType
+ALU = mybir.AluOpType
+
+D, T, I, Q, E, M = 512, 1024, 512, 512, 512, 1024
+P = 128
+PACK = 4
+BANK = 512
+CHUNK = 256
+CHUNKS = I // CHUNK
+FLOPS = 2 * D * Q * T + 2 * Q * E * I
+
+SCORE_BANKS = 6
+FADE_BANK = 2
+SUM_BANK = (6, 0)
+VECTOR_EMPTIES = {(1, 1)}
+VECTOR_SCATTERS = {(3, 0)}
+
+
+def tile_attend_difference_delivered_lean_kernel(tc, query, keys_words, keys_scales, qs, msgs, old, fade, offs, offs2, offs3, out):
+    nc = tc.nc
+    with ExitStack() as ctx:
+        keep = ctx.enter_context(tc.tile_pool(name="keep", bufs=1))
+        psum = ctx.enter_context(tc.psum_pool(name="psum", bufs=1))
+        banks = [psum.tile([P, BANK], F32, name=f"bank{b}") for b in range(8)]
+
+        half = Q // 2
+        q_rows = query.rearrange("(p j) q -> p j q", j=PACK)
+        q_raw = [keep.tile([P, PACK, half], F32, name=f"q_raw{h}") for h in range(2)]
+        k_words = [keep.tile([P, BANK], U32, name=f"k_words{b}", align_bytes=64) for b in range(T // BANK)]
+        k_scales = keep.tile([P, T], U8, align_bytes=64)
+        nc.vector.memset(k_scales[:].bitcast(U32), 0)
+        for h in range(2):
+            nc.sync.dma_start(out=q_raw[h][:], in_=q_rows[:, :, h * half : (h + 1) * half])
+        for quad in range(4):
+            nc.sync.dma_start(
+                out=k_scales[32 * quad : 32 * quad + 4, :].bitcast(I32),
+                in_=keys_scales[0, 4 * quad : 4 * quad + 4, :].bitcast(I32),
+            )
+        word_rows = keys_words[0].rearrange("p n t -> p (n t)").bitcast(I32)
+        for b in range(T // BANK):
+            nc.sync.dma_start(out=k_words[b][:].bitcast(I32), in_=word_rows[:, b * BANK : (b + 1) * BANK])
+        list2 = keep.tile([P, I // 16], U16)
+        nc.sync.dma_start(list2[:], offs2)
+        list1 = keep.tile([P, I // 16], U16)
+        nc.sync.dma_start(list1[:], offs)
+        m_raw = keep.tile([P, PACK, E], F32)
+        nc.sync.dma_start(out=m_raw[:], in_=msgs.rearrange("(p j) e -> p j e", j=PACK))
+        qs_cols = keep.tile([P, PACK], F32)
+        nc.sync.dma_start(out=qs_cols[:], in_=qs.rearrange("(p r) o -> p (r o)", r=PACK))
+        result = [keep.tile([P, M], F32, name=f"result{e}") for e in range(4)]
+        for e in range(4):
+            nc.sync.dma_start(out=result[e][:], in_=old[e * P : (e + 1) * P, :])
+        list3 = keep.tile([P, I // 16], U16)
+        nc.sync.dma_start(list3[:], offs3)
+
+        identity = keep.tile([P, P], F32)
+        make_identity(nc, identity[:])
+
+        windows = [keep.tile([P, M], F32, name=f"window{e}") for e in range(4)]
+        for e in range(4):
+            nc.vector.memset(windows[e][:], 0.0)
+
+        fade_rows = []
+
+        def spread_fade():
+            fade_cols = m_raw[:, 0, 0 : 2 * PACK].rearrange("p (h b) -> p h b", h=2)
+            nc.sync.dma_start(out=fade_cols, in_=fade.rearrange("o (h p b) -> p (o h) b", h=2, b=PACK))
+            for h in range(2):
+                fade_rows.append(banks[FADE_BANK + h][:].rearrange("p (b s) -> p b s", b=PACK))
+                for b in range(PACK):
+                    nc.tensor.transpose(fade_rows[h][:, b, :], fade_cols[:, h, b : b + 1].to_broadcast([P, P]), identity[:])
+
+        q_grouped = keep.tile([P, PACK, P, PACK], BF16, align_bytes=64)
+        for h, s0, s1, copy in ((0, 0, 64, nc.vector.tensor_copy), (1, 0, 40, nc.vector.tensor_copy), (1, 40, 64, nc.scalar.copy)):
+            copy(
+                q_grouped[:, :, 64 * h + s0 : 64 * h + s1, :].rearrange("p r s j -> p s j r"),
+                q_raw[h][:, :, PACK * s0 : PACK * s1].rearrange("p j (s r) -> p s j r", r=PACK),
+            )
+        q_codes = keep.tile([P, Q], U32, align_bytes=64)
+        q_scales = keep.tile([P, Q], U8, align_bytes=64)
+        for r0, r1 in ((0, 1), (1, 2), (2, 4)):
+            cols = slice(r0 * P, r1 * P)
+            nc.vector.quantize_mx(
+                out=q_codes[:, cols].bitcast(FP8X4),
+                scales=q_scales[:, cols],
+                in_=q_grouped[:, r0:r1].rearrange("p r s j -> p (r s j)"),
+            )
+
+        scores = [keep.tile([P, T], F32, name=f"scores{r}") for r in range(PACK)]
+        stages = [keep.tile([P, PACK, CHUNK], F32, name=f"stage{k}", align_bytes=64) for k in range(3)]
+        w_grouped = keep.tile([P, CHUNKS, CHUNK, PACK], BF16, align_bytes=64)
+        w_codes = keep.tile([P, I], U32, align_bytes=64)
+        w_scales = keep.tile([P, I], U8, align_bytes=64)
+        sums = keep.tile([P, CHUNKS, 4, CHUNK], F32)
+
+        def entries(lst, c):
+            return lst[:, c * (CHUNK // 16) : (c + 1) * (CHUNK // 16)]
+
+        def score(r):
+            rows = slice(r * P, (r + 1) * P)
+            for b in range(T // BANK):
+                cols = slice(b * BANK, (b + 1) * BANK)
+                bank = banks[(2 * r + b) % SCORE_BANKS]
+                nc.tensor.matmul_mx(
+                    out=bank[:],
+                    lhsT=q_codes[:, rows].bitcast(FP8X4),
+                    lhsT_scale=q_scales[:, rows],
+                    rhs=k_words[b][:].bitcast(FP8X4),
+                    rhs_scale=k_scales[:, cols],
+                    start=True,
+                    stop=True,
+                )
+                if b == 0:
+                    nc.scalar.copy(scores[r][:, cols], bank[:])
+                else:
+                    nc.vector.tensor_copy(scores[r][:, cols], bank[:])
+
+        def weigh(r, c, steps="gds"):
+            picked = stages[c][:, r, :]
+            diff = stages[c + 1][:, r, :]
+            if "g" in steps:
+                nc.scalar.activation(picked, scores[r][:].indirect(entries(list2, c)), ACT.Copy)
+            if "d" in steps:
+                nc.vector.tensor_tensor(diff, scores[r][:].indirect(entries(list1, c)), picked, ALU.subtract)
+
+        def squash(c):
+            nc.scalar.activation(stages[(c + 2) % 3][:], stages[c + 1][:], ACT.Sigmoid)
+
+        def carry(c):
+            nc.vector.tensor_tensor(
+                w_grouped[:, c].rearrange("p (g i) r -> p g r i", i=4),
+                stages[(c + 2) % 3][:].rearrange("p r (g i) -> p g r i", i=4),
+                qs_cols[:].unsqueeze(1).unsqueeze(3).to_broadcast([P, CHUNK // 4, PACK, 4]),
+                ALU.mult,
+            )
+            cols = slice(c * CHUNK, (c + 1) * CHUNK)
+            nc.vector.quantize_mx(
+                out=w_codes[:, cols].bitcast(FP8X4),
+                scales=w_scales[:, cols],
+                in_=w_grouped[:, c].rearrange("p i r -> p (i r)"),
+            )
+            for pair in range(2):
+                bank = banks[SUM_BANK[c] + pair][:].rearrange("p (k i) -> p k i", k=2)
+                for k in range(2):
+                    rows = slice((2 * pair + k) * P, (2 * pair + k + 1) * P)
+                    nc.tensor.matmul_mx(
+                        out=bank[:, k, :],
+                        lhsT=m_codes[:, rows].bitcast(FP8X4),
+                        lhsT_scale=m_scales[:, rows],
+                        rhs=w_codes[:, cols].bitcast(FP8X4),
+                        rhs_scale=w_scales[:, cols],
+                        start=True,
+                        stop=True,
+                    )
+                if (c, pair) not in VECTOR_EMPTIES:
+                    nc.scalar.copy(sums[:, c, 2 * pair : 2 * pair + 2, :], bank)
+                else:
+                    nc.vector.tensor_copy(sums[:, c, 2 * pair : 2 * pair + 2, :], bank)
+
+        def scatter(e, c):
+            places = windows[e][:].indirect(entries(list3, c))
+            if (e, c) in VECTOR_SCATTERS:
+                nc.vector.tensor_copy(places, sums[:, c, e, :])
+            else:
+                nc.scalar.activation(places, sums[:, c, e, :], ACT.Copy)
+
+        def fading(e):
+            for h in range(2):
+                part = result[e][:, h * BANK : (h + 1) * BANK].rearrange("p (s b) -> p s b", b=PACK)
+                nc.vector.tensor_tensor(part, part, fade_rows[h].rearrange("p b s -> p s b"), ALU.mult)
+
+        def finish(e):
+            pieces = 4 if e == 3 else 2
+            for h in range(pieces):
+                cols = slice(h * M // pieces, (h + 1) * M // pieces)
+                nc.vector.tensor_tensor(result[e][:, cols], result[e][:, cols], windows[e][:, cols], ALU.add)
+                nc.sync.dma_start(out=out[e * P : (e + 1) * P, cols], in_=result[e][:, cols])
+
+        m_grouped = stages[0][:].rearrange("p r i -> p (r i)").bitcast(BF16)
+        m_codes = keep.tile([P, E], U32, align_bytes=64)
+        m_scales = keep.tile([P, E], U8, align_bytes=64)
+
+        def quantise_msgs():
+            nc.vector.tensor_copy(
+                out=m_grouped.rearrange("p (g i j) -> p g j i", i=4, j=PACK),
+                in_=m_raw[:].rearrange("p j (g i) -> p g j i", i=4),
+            )
+            nc.vector.quantize_mx(out=m_codes[:].bitcast(FP8X4), scales=m_scales[:], in_=m_grouped)
+
+        for r in range(PACK):
+            score(r)
+            weigh(r, 0)
+        squash(0)
+        quantise_msgs()
+        carry(0)
+        spread_fade()
+        for r in range(PACK):
+            weigh(r, 1)
+        scatter(0, 0)
+        squash(1)
+        carry(1)
+        scatter(1, 0)
+        scatter(2, 0)
+        for e in range(4):
+            fading(e)
+        scatter(3, 0)
+        for e in range(4):
+            scatter(e, 1)
+            finish(e)

@@ -18,14 +18,9 @@ P = 128
 PACK = 4
 BANK = 512
 CHUNK = 256
-CHUNKS = I // CHUNK
 FLOPS = 2 * D * Q * T + 2 * Q * E * I
-
-SCORE_BANKS = 6
-FADE_BANK = 2
-SUM_BANK = (6, 0)
-VECTOR_EMPTIES = {(1, 1)}
-VECTOR_SCATTERS = {(3, 0)}
+TAIL = 96
+SPLIT = 128
 
 
 def tile_attend_difference_delivered_lean_kernel(tc, query, keys_words, keys_scales, qs, msgs, old, fade, offs, offs2, offs3, out):
@@ -38,9 +33,20 @@ def tile_attend_difference_delivered_lean_kernel(tc, query, keys_words, keys_sca
         half = Q // 2
         q_rows = query.rearrange("(p j) q -> p j q", j=PACK)
         q_raw = [keep.tile([P, PACK, half], F32, name=f"q_raw{h}") for h in range(2)]
-        k_words = [keep.tile([P, BANK], U32, name=f"k_words{b}", align_bytes=64) for b in range(T // BANK)]
+        k_words = keep.tile([P, T], U32, align_bytes=64)
         k_scales = keep.tile([P, T], U8, align_bytes=64)
-        nc.vector.memset(k_scales[:].bitcast(U32), 0)
+        q_grouped = keep.tile([P, PACK, P, PACK], BF16, align_bytes=64)
+        fade_cols = q_grouped[:, PACK - 1, P - PACK :, :].rearrange("p s j -> p (s j)").bitcast(F32)
+        list1 = keep.tile([P, I // 16], U16)
+        list2 = keep.tile([P, I // 16], U16)
+        list3 = keep.tile([P, I // 16], U16)
+        m_raw = keep.tile([P, PACK, E], F32)
+        qs_cols = keep.tile([P, PACK], F32)
+        held = {e: keep.tile([P, M], F32, name=f"held{e}") for e in (0, 2, 3)}
+        result = [held[0][:], m_raw[:, 0:2, :].rearrange("p j e -> p (j e)"), held[2][:], held[3][:]]
+
+        nc.gpsimd.memset(k_scales[:].bitcast(U32), 0)
+        nc.sync.dma_start(out=fade_cols, in_=fade.rearrange("o (p b) -> p (o b)", b=2 * PACK))
         for h in range(2):
             nc.sync.dma_start(out=q_raw[h][:], in_=q_rows[:, :, h * half : (h + 1) * half])
         for quad in range(4):
@@ -48,42 +54,40 @@ def tile_attend_difference_delivered_lean_kernel(tc, query, keys_words, keys_sca
                 out=k_scales[32 * quad : 32 * quad + 4, :].bitcast(I32),
                 in_=keys_scales[0, 4 * quad : 4 * quad + 4, :].bitcast(I32),
             )
-        word_rows = keys_words[0].rearrange("p n t -> p (n t)").bitcast(I32)
-        for b in range(T // BANK):
-            nc.sync.dma_start(out=k_words[b][:].bitcast(I32), in_=word_rows[:, b * BANK : (b + 1) * BANK])
-        list2 = keep.tile([P, I // 16], U16)
+        nc.sync.dma_start(out=k_words[:].bitcast(I32), in_=keys_words[0].rearrange("p n t -> p (n t)").bitcast(I32))
+        nc.sync.dma_start(out=result[0], in_=old[0:P, :])
         nc.sync.dma_start(list2[:], offs2)
-        list1 = keep.tile([P, I // 16], U16)
         nc.sync.dma_start(list1[:], offs)
-        m_raw = keep.tile([P, PACK, E], F32)
         nc.sync.dma_start(out=m_raw[:], in_=msgs.rearrange("(p j) e -> p j e", j=PACK))
-        qs_cols = keep.tile([P, PACK], F32)
         nc.sync.dma_start(out=qs_cols[:], in_=qs.rearrange("(p r) o -> p (r o)", r=PACK))
-        result = [keep.tile([P, M], F32, name=f"result{e}") for e in range(4)]
-        for e in range(4):
-            nc.sync.dma_start(out=result[e][:], in_=old[e * P : (e + 1) * P, :])
-        list3 = keep.tile([P, I // 16], U16)
         nc.sync.dma_start(list3[:], offs3)
+        for e in (3, 2):
+            nc.sync.dma_start(out=result[e], in_=old[e * P : (e + 1) * P, :])
 
         identity = keep.tile([P, P], F32)
         make_identity(nc, identity[:])
 
         windows = [keep.tile([P, M], F32, name=f"window{e}") for e in range(4)]
         for e in range(4):
-            nc.vector.memset(windows[e][:], 0.0)
+            nc.vector.memset(windows[e][:].bitcast(I32), 0)
 
-        fade_rows = []
+        def by_bank(row, h):
+            return row.rearrange("p (s h b) -> p h s b", h=2, b=PACK)[:, h]
 
-        def spread_fade():
-            fade_cols = m_raw[:, 0, 0 : 2 * PACK].rearrange("p (h b) -> p h b", h=2)
-            nc.sync.dma_start(out=fade_cols, in_=fade.rearrange("o (h p b) -> p (o h) b", h=2, b=PACK))
+        fade_wide = keep.tile([P, M], F32)
+        fade_rows = [banks[6 + h][:].rearrange("p (b s) -> p s b", b=PACK) for h in range(2)]
+
+        def spread_fade(first_bank):
             for h in range(2):
-                fade_rows.append(banks[FADE_BANK + h][:].rearrange("p (b s) -> p b s", b=PACK))
                 for b in range(PACK):
-                    nc.tensor.transpose(fade_rows[h][:, b, :], fade_cols[:, h, b : b + 1].to_broadcast([P, P]), identity[:])
+                    column = fade_cols[:, PACK * h + b : PACK * h + b + 1]
+                    nc.tensor.transpose(banks[first_bank + h][:, b * P : (b + 1) * P], column.to_broadcast([P, P]), identity[:])
 
-        q_grouped = keep.tile([P, PACK, P, PACK], BF16, align_bytes=64)
-        for h, s0, s1, copy in ((0, 0, 64, nc.vector.tensor_copy), (1, 0, 40, nc.vector.tensor_copy), (1, 40, 64, nc.scalar.copy)):
+        spread_fade(6)
+        for h in range(2):
+            nc.scalar.copy(by_bank(fade_wide[:], h), fade_rows[h])
+
+        for h, s0, s1, copy in ((0, 0, 64, nc.vector.tensor_copy), (1, 0, 64, nc.vector.tensor_copy)):
             copy(
                 q_grouped[:, :, 64 * h + s0 : 64 * h + s1, :].rearrange("p r s j -> p s j r"),
                 q_raw[h][:, :, PACK * s0 : PACK * s1].rearrange("p j (s r) -> p s j r", r=PACK),
@@ -100,24 +104,31 @@ def tile_attend_difference_delivered_lean_kernel(tc, query, keys_words, keys_sca
 
         scores = [keep.tile([P, T], F32, name=f"scores{r}") for r in range(PACK)]
         stages = [keep.tile([P, PACK, CHUNK], F32, name=f"stage{k}", align_bytes=64) for k in range(3)]
-        w_grouped = keep.tile([P, CHUNKS, CHUNK, PACK], BF16, align_bytes=64)
+        early = keep.tile([P, CHUNK, PACK], BF16, align_bytes=64)
+        late = keep.tile([P, M + CHUNK], F32, align_bytes=64)
+        w_grouped = [early[:], late[:, M - CHUNK :].bitcast(BF16).rearrange("p (i r) -> p i r", r=PACK)]
         w_codes = keep.tile([P, I], U32, align_bytes=64)
         w_scales = keep.tile([P, I], U8, align_bytes=64)
-        sums = keep.tile([P, CHUNKS, 4, CHUNK], F32)
+        sum_tile = keep.tile([P, 7, CHUNK], F32)
+        sums = [[sum_tile[:, 0, :], sum_tile[:, 1, :], sum_tile[:, 2, :], late[:, M:]], [sum_tile[:, 3 + e, :] for e in range(4)]]
+        m_grouped = stages[0][:].rearrange("p r i -> p (r i)").bitcast(BF16)
+        m_codes = keep.tile([P, E], U32, align_bytes=64)
+        m_scales = keep.tile([P, E], U8, align_bytes=64)
+        faded = [result[0], result[1], late[:, 0:M], stages[1][:].rearrange("p r i -> p (r i)")]
 
-        def entries(lst, c):
-            return lst[:, c * (CHUNK // 16) : (c + 1) * (CHUNK // 16)]
+        def entries(lst, start, count):
+            return lst[:, start // 16 : (start + count) // 16]
 
         def score(r):
             rows = slice(r * P, (r + 1) * P)
             for b in range(T // BANK):
                 cols = slice(b * BANK, (b + 1) * BANK)
-                bank = banks[(2 * r + b) % SCORE_BANKS]
+                bank = banks[(2 * r + b) % 6]
                 nc.tensor.matmul_mx(
                     out=bank[:],
                     lhsT=q_codes[:, rows].bitcast(FP8X4),
                     lhsT_scale=q_scales[:, rows],
-                    rhs=k_words[b][:].bitcast(FP8X4),
+                    rhs=k_words[:, cols].bitcast(FP8X4),
                     rhs_scale=k_scales[:, cols],
                     start=True,
                     stop=True,
@@ -127,70 +138,14 @@ def tile_attend_difference_delivered_lean_kernel(tc, query, keys_words, keys_sca
                 else:
                     nc.vector.tensor_copy(scores[r][:, cols], bank[:])
 
-        def weigh(r, c, steps="gds"):
-            picked = stages[c][:, r, :]
-            diff = stages[c + 1][:, r, :]
-            if "g" in steps:
-                nc.scalar.activation(picked, scores[r][:].indirect(entries(list2, c)), ACT.Copy)
-            if "d" in steps:
-                nc.vector.tensor_tensor(diff, scores[r][:].indirect(entries(list1, c)), picked, ALU.subtract)
+        def pick(r, c):
+            nc.scalar.activation(stages[c][:, r, :], scores[r][:].indirect(entries(list2, c * CHUNK, CHUNK)), ACT.Copy)
+
+        def differ(r, c):
+            nc.vector.tensor_tensor(stages[c + 1][:, r, :], scores[r][:].indirect(entries(list1, c * CHUNK, CHUNK)), stages[c][:, r, :], ALU.subtract)
 
         def squash(c):
             nc.scalar.activation(stages[(c + 2) % 3][:], stages[c + 1][:], ACT.Sigmoid)
-
-        def carry(c):
-            nc.vector.tensor_tensor(
-                w_grouped[:, c].rearrange("p (g i) r -> p g r i", i=4),
-                stages[(c + 2) % 3][:].rearrange("p r (g i) -> p g r i", i=4),
-                qs_cols[:].unsqueeze(1).unsqueeze(3).to_broadcast([P, CHUNK // 4, PACK, 4]),
-                ALU.mult,
-            )
-            cols = slice(c * CHUNK, (c + 1) * CHUNK)
-            nc.vector.quantize_mx(
-                out=w_codes[:, cols].bitcast(FP8X4),
-                scales=w_scales[:, cols],
-                in_=w_grouped[:, c].rearrange("p i r -> p (i r)"),
-            )
-            for pair in range(2):
-                bank = banks[SUM_BANK[c] + pair][:].rearrange("p (k i) -> p k i", k=2)
-                for k in range(2):
-                    rows = slice((2 * pair + k) * P, (2 * pair + k + 1) * P)
-                    nc.tensor.matmul_mx(
-                        out=bank[:, k, :],
-                        lhsT=m_codes[:, rows].bitcast(FP8X4),
-                        lhsT_scale=m_scales[:, rows],
-                        rhs=w_codes[:, cols].bitcast(FP8X4),
-                        rhs_scale=w_scales[:, cols],
-                        start=True,
-                        stop=True,
-                    )
-                if (c, pair) not in VECTOR_EMPTIES:
-                    nc.scalar.copy(sums[:, c, 2 * pair : 2 * pair + 2, :], bank)
-                else:
-                    nc.vector.tensor_copy(sums[:, c, 2 * pair : 2 * pair + 2, :], bank)
-
-        def scatter(e, c):
-            places = windows[e][:].indirect(entries(list3, c))
-            if (e, c) in VECTOR_SCATTERS:
-                nc.vector.tensor_copy(places, sums[:, c, e, :])
-            else:
-                nc.scalar.activation(places, sums[:, c, e, :], ACT.Copy)
-
-        def fading(e):
-            for h in range(2):
-                part = result[e][:, h * BANK : (h + 1) * BANK].rearrange("p (s b) -> p s b", b=PACK)
-                nc.vector.tensor_tensor(part, part, fade_rows[h].rearrange("p b s -> p s b"), ALU.mult)
-
-        def finish(e):
-            pieces = 4 if e == 3 else 2
-            for h in range(pieces):
-                cols = slice(h * M // pieces, (h + 1) * M // pieces)
-                nc.vector.tensor_tensor(result[e][:, cols], result[e][:, cols], windows[e][:, cols], ALU.add)
-                nc.sync.dma_start(out=out[e * P : (e + 1) * P, cols], in_=result[e][:, cols])
-
-        m_grouped = stages[0][:].rearrange("p r i -> p (r i)").bitcast(BF16)
-        m_codes = keep.tile([P, E], U32, align_bytes=64)
-        m_scales = keep.tile([P, E], U8, align_bytes=64)
 
         def quantise_msgs():
             nc.vector.tensor_copy(
@@ -199,23 +154,93 @@ def tile_attend_difference_delivered_lean_kernel(tc, query, keys_words, keys_sca
             )
             nc.vector.quantize_mx(out=m_codes[:].bitcast(FP8X4), scales=m_scales[:], in_=m_grouped)
 
+        def carry(c):
+            nc.vector.tensor_tensor(
+                w_grouped[c].rearrange("p (g i) r -> p g r i", i=4),
+                stages[(c + 2) % 3][:].rearrange("p r (g i) -> p g r i", i=4),
+                qs_cols[:].unsqueeze(1).unsqueeze(3).to_broadcast([P, CHUNK // 4, PACK, 4]),
+                ALU.mult,
+            )
+            cols = slice(c * CHUNK, (c + 1) * CHUNK)
+            nc.vector.quantize_mx(
+                out=w_codes[:, cols].bitcast(FP8X4),
+                scales=w_scales[:, cols],
+                in_=w_grouped[c].rearrange("p i r -> p (i r)"),
+            )
+            for e in range(4):
+                rows = slice(e * P, (e + 1) * P)
+                nc.tensor.matmul_mx(
+                    out=products(c, e, 1),
+                    lhsT=m_codes[:, rows].bitcast(FP8X4),
+                    lhsT_scale=m_scales[:, rows],
+                    rhs=w_codes[:, cols].bitcast(FP8X4),
+                    rhs_scale=w_scales[:, cols],
+                    start=True,
+                    stop=True,
+                )
+
+        def products(c, e, count):
+            return banks[2 + 2 * c + e // 2][:, (e % 2) * CHUNK : (e % 2 + count) * CHUNK]
+
+        def pair(c, e):
+            first = 3 * c + e
+            return sum_tile[:, first : first + 2, :].rearrange("p k i -> p (k i)")
+
+        def scatter(e, c, start, count, on_vector):
+            places = windows[e][:].indirect(entries(list3, c * CHUNK + start, count))
+            values = sums[c][e][:, start : start + count]
+            if on_vector:
+                nc.vector.tensor_copy(places, values)
+            else:
+                nc.scalar.activation(places, values, ACT.Copy)
+
+        def finish(e, pieces):
+            for h in range(pieces):
+                cols = slice(h * M // pieces, (h + 1) * M // pieces)
+                nc.vector.tensor_tensor(result[e][:, cols], faded[e][:, cols], windows[e][:, cols], ALU.add)
+                nc.sync.dma_start(out=out[e * P : (e + 1) * P, cols], in_=result[e][:, cols])
+
+        def fading_gpsimd(e, stop):
+            nc.gpsimd.tensor_tensor(faded[e][:, 0:stop], result[e][:, 0:stop], fade_wide[:, 0:stop], ALU.mult)
+
+        def fading_vector(e, s0):
+            for h in range(2):
+                nc.vector.tensor_tensor(by_bank(faded[e], h)[:, s0:, :], by_bank(result[e], h)[:, s0:, :], fade_rows[h][:, s0:, :], ALU.mult)
+
+        fading_gpsimd(0, M)
         for r in range(PACK):
             score(r)
-            weigh(r, 0)
+            pick(r, 0)
+            if r == PACK - 2:
+                differ(0, 0)
+        for r in range(1, PACK):
+            differ(r, 0)
         squash(0)
         quantise_msgs()
+        nc.sync.dma_start(out=result[1], in_=old[P : 2 * P, :])
         carry(0)
-        spread_fade()
+        nc.scalar.copy(pair(0, 0), products(0, 0, 2))
         for r in range(PACK):
-            weigh(r, 1)
-        scatter(0, 0)
+            pick(r, 1)
+            differ(r, 1)
+        scatter(0, 0, 0, CHUNK, False)
         squash(1)
+        fading_gpsimd(3, 2 * PACK * TAIL)
         carry(1)
-        scatter(1, 0)
-        scatter(2, 0)
-        for e in range(4):
-            fading(e)
-        scatter(3, 0)
-        for e in range(4):
-            scatter(e, 1)
-            finish(e)
+        nc.vector.tensor_copy(sums[0][2], products(0, 2, 1))
+        fading_vector(1, 0)
+        fading_vector(3, TAIL)
+        scatter(1, 0, 0, CHUNK, False)
+        scatter(2, 0, 0, CHUNK, False)
+        nc.vector.tensor_copy(sums[0][3], products(0, 3, 1))
+        scatter(3, 0, 0, CHUNK, True)
+        fading_gpsimd(2, M)
+        nc.scalar.copy(pair(1, 0), products(1, 0, 2))
+        nc.vector.tensor_copy(pair(1, 2), products(1, 2, 2))
+        scatter(3, 1, 0, CHUNK, True)
+        for e in range(3):
+            scatter(e, 1, 0, CHUNK, False)
+        finish(0, 2)
+        finish(3, 2)
+        finish(1, 2)
+        finish(2, 4)

@@ -105,12 +105,12 @@ def tile_attend_difference_delivered_lean_kernel(tc, query, keys_words, keys_sca
         scores = [keep.tile([P, T], F32, name=f"scores{r}") for r in range(PACK)]
         stages = [keep.tile([P, PACK, CHUNK], F32, name=f"stage{k}", align_bytes=64) for k in range(3)]
         early = keep.tile([P, CHUNK, PACK], BF16, align_bytes=64)
-        late = keep.tile([P, M + CHUNK], F32, align_bytes=64)
-        w_grouped = [early[:], late[:, M - CHUNK :].bitcast(BF16).rearrange("p (i r) -> p i r", r=PACK)]
+        late = keep.tile([P, M], F32, align_bytes=64)
+        w_grouped = [early[:], late[:, M // 2 :].bitcast(BF16).rearrange("p (i r) -> p i r", r=PACK)]
         w_codes = keep.tile([P, I], U32, align_bytes=64)
         w_scales = keep.tile([P, I], U8, align_bytes=64)
-        sum_tile = keep.tile([P, 7, CHUNK], F32)
-        sums = [[sum_tile[:, 0, :], sum_tile[:, 1, :], sum_tile[:, 2, :], late[:, M:]], [sum_tile[:, 3 + e, :] for e in range(4)]]
+        sum_tile = keep.tile([P, 8, CHUNK], F32)
+        sums = [[sum_tile[:, 4 * c + e, :] for e in range(4)] for c in range(2)]
         m_grouped = stages[0][:].rearrange("p r i -> p (r i)").bitcast(BF16)
         m_codes = keep.tile([P, E], U32, align_bytes=64)
         m_scales = keep.tile([P, E], U8, align_bytes=64)
@@ -133,12 +133,15 @@ def tile_attend_difference_delivered_lean_kernel(tc, query, keys_words, keys_sca
                     start=True,
                     stop=True,
                 )
-                if b == 0:
+                if b == 0 and r not in (2,):
                     nc.scalar.copy(scores[r][:, cols], bank[:])
                 else:
                     nc.vector.tensor_copy(scores[r][:, cols], bank[:])
 
-        def pick(r, c):
+        def pick(r, c, on_vector=False):
+            if on_vector:
+                nc.vector.tensor_copy(stages[c][:, r, :], scores[r][:].indirect(entries(list2, c * CHUNK, CHUNK)))
+                return
             nc.scalar.activation(stages[c][:, r, :], scores[r][:].indirect(entries(list2, c * CHUNK, CHUNK)), ACT.Copy)
 
         def differ(r, c):
@@ -167,7 +170,7 @@ def tile_attend_difference_delivered_lean_kernel(tc, query, keys_words, keys_sca
                 scales=w_scales[:, cols],
                 in_=w_grouped[c].rearrange("p i r -> p (i r)"),
             )
-            for e in range(4):
+            for e in ((0, 1, 2, 3), (2, 3, 0, 1))[c]:
                 rows = slice(e * P, (e + 1) * P)
                 nc.tensor.matmul_mx(
                     out=products(c, e, 1),
@@ -183,7 +186,7 @@ def tile_attend_difference_delivered_lean_kernel(tc, query, keys_words, keys_sca
             return banks[2 + 2 * c + e // 2][:, (e % 2) * CHUNK : (e % 2 + count) * CHUNK]
 
         def pair(c, e):
-            first = 3 * c + e
+            first = 4 * c + e
             return sum_tile[:, first : first + 2, :].rearrange("p k i -> p (k i)")
 
         def scatter(e, c, start, count, on_vector):
@@ -219,28 +222,27 @@ def tile_attend_difference_delivered_lean_kernel(tc, query, keys_words, keys_sca
         quantise_msgs()
         nc.sync.dma_start(out=result[1], in_=old[P : 2 * P, :])
         carry(0)
-        nc.scalar.copy(pair(0, 0), products(0, 0, 2))
+        nc.scalar.copy(sums[0][0], products(0, 0, 1))
         for r in range(PACK):
-            pick(r, 1)
+            pick(r, 1, r in ())
             differ(r, 1)
         scatter(0, 0, 0, CHUNK, False)
         squash(1)
         fading_gpsimd(3, 2 * PACK * TAIL)
         carry(1)
-        nc.vector.tensor_copy(sums[0][2], products(0, 2, 1))
+        nc.vector.tensor_copy(pair(0, 2), products(0, 2, 2))
+        nc.vector.tensor_copy(sums[0][1], products(0, 1, 1))
         fading_vector(1, 0)
         fading_vector(3, TAIL)
-        scatter(1, 0, 0, CHUNK, False)
-        scatter(2, 0, 0, CHUNK, False)
-        nc.vector.tensor_copy(sums[0][3], products(0, 3, 1))
-        scatter(3, 0, 0, CHUNK, True)
+        for e in (3, 1, 2):
+            scatter(e, 0, 0, CHUNK, False)
         fading_gpsimd(2, M)
-        nc.scalar.copy(pair(1, 0), products(1, 0, 2))
         nc.vector.tensor_copy(pair(1, 2), products(1, 2, 2))
+        nc.vector.tensor_copy(pair(1, 0), products(1, 0, 2))
         scatter(3, 1, 0, CHUNK, True)
-        for e in range(3):
+        for e in (2, 0, 1):
             scatter(e, 1, 0, CHUNK, False)
-        finish(0, 2)
         finish(3, 2)
-        finish(1, 2)
-        finish(2, 4)
+        finish(2, 2)
+        finish(0, 2)
+        finish(1, 4)

from contextlib import ExitStack

import concourse.mybir as mybir
from concourse.masks import make_identity

F32 = mybir.dt.float32
BF16 = mybir.dt.bfloat16
I32 = mybir.dt.int32
U32 = mybir.dt.uint32
U16 = mybir.dt.uint16
U8 = mybir.dt.uint8
FP8X4 = mybir.dt.float8_e4m3fn_x4
ACT = mybir.ActivationFunctionType
ALU = mybir.AluOpType

D, T, I, Q, E, M = 512, 1024, 512, 512, 512, 1024
P = 128
PACK = 4
BANK = 512
CHUNK = 256
FLOPS = 2 * D * Q * T + 2 * Q * E * I
TAIL = 96
SPLIT = 128


def tile_attend_difference_delivered_lean_kernel(tc, query, keys_words, keys_scales, qs, msgs, old, fade, offs, offs2, offs3, out):
    nc = tc.nc
    with ExitStack() as ctx:
        keep = ctx.enter_context(tc.tile_pool(name="keep", bufs=1))
        psum = ctx.enter_context(tc.psum_pool(name="psum", bufs=1))
        banks = [psum.tile([P, BANK], F32, name=f"bank{b}") for b in range(8)]

        half = Q // 2
        q_rows = query.rearrange("(p j) q -> p j q", j=PACK)
        q_raw = [keep.tile([P, PACK, half], F32, name=f"q_raw{h}") for h in range(2)]
        k_words = keep.tile([P, T], U32, align_bytes=64)
        k_scales = keep.tile([P, T], U8, align_bytes=64)
        q_grouped = keep.tile([P, PACK, P, PACK], BF16, align_bytes=64)
        fade_cols = q_grouped[:, PACK - 1, P - PACK :, :].rearrange("p s j -> p (s j)").bitcast(F32)
        list1 = keep.tile([P, I // 16], U16)
        list2 = keep.tile([P, I // 16], U16)
        list3 = keep.tile([P, I // 16], U16)
        m_raw = keep.tile([P, PACK, E], F32)
        qs_cols = keep.tile([P, PACK], F32)
        held = {e: keep.tile([P, M], F32, name=f"held{e}") for e in (0, 2, 3)}
        result = [held[0][:], m_raw[:, 0:2, :].rearrange("p j e -> p (j e)"), held[2][:], held[3][:]]

        nc.gpsimd.memset(k_scales[:].bitcast(U32), 0)
        nc.sync.dma_start(out=fade_cols, in_=fade.rearrange("o (p b) -> p (o b)", b=2 * PACK))
        for h in range(2):
            nc.sync.dma_start(out=q_raw[h][:], in_=q_rows[:, :, h * half : (h + 1) * half])
        for quad in range(4):
            nc.sync.dma_start(
                out=k_scales[32 * quad : 32 * quad + 4, :].bitcast(I32),
                in_=keys_scales[0, 4 * quad : 4 * quad + 4, :].bitcast(I32),
            )
        nc.sync.dma_start(out=k_words[:].bitcast(I32), in_=keys_words[0].rearrange("p n t -> p (n t)").bitcast(I32))
        nc.sync.dma_start(out=result[0], in_=old[0:P, :])
        nc.sync.dma_start(list2[:], offs2)
        nc.sync.dma_start(list1[:], offs)
        nc.sync.dma_start(out=m_raw[:], in_=msgs.rearrange("(p j) e -> p j e", j=PACK))
        nc.sync.dma_start(out=qs_cols[:], in_=qs.rearrange("(p r) o -> p (r o)", r=PACK))
        nc.sync.dma_start(list3[:], offs3)
        for e in (3, 2):
            nc.sync.dma_start(out=result[e], in_=old[e * P : (e + 1) * P, :])

        identity = keep.tile([P, P], F32)
        make_identity(nc, identity[:])

        windows = [keep.tile([P, M], F32, name=f"window{e}") for e in range(4)]
        for e in range(4):
            nc.vector.memset(windows[e][:].bitcast(I32), 0)

        def by_bank(row, h):
            return row.rearrange("p (s h b) -> p h s b", h=2, b=PACK)[:, h]

        fade_wide = keep.tile([P, M], F32)
        fade_rows = [banks[6 + h][:].rearrange("p (b s) -> p s b", b=PACK) for h in range(2)]

        def spread_fade(first_bank):
            for h in range(2):
                for b in range(PACK):
                    column = fade_cols[:, PACK * h + b : PACK * h + b + 1]
                    nc.tensor.transpose(banks[first_bank + h][:, b * P : (b + 1) * P], column.to_broadcast([P, P]), identity[:])

        spread_fade(6)
        for h in range(2):
            nc.scalar.copy(by_bank(fade_wide[:], h), fade_rows[h])

        for h, s0, s1, copy in ((0, 0, 64, nc.vector.tensor_copy), (1, 0, 64, nc.vector.tensor_copy)):
            copy(
                q_grouped[:, :, 64 * h + s0 : 64 * h + s1, :].rearrange("p r s j -> p s j r"),
                q_raw[h][:, :, PACK * s0 : PACK * s1].rearrange("p j (s r) -> p s j r", r=PACK),
            )
        q_codes = keep.tile([P, Q], U32, align_bytes=64)
        q_scales = keep.tile([P, Q], U8, align_bytes=64)
        for r0, r1 in ((0, 1), (1, 2), (2, 4)):
            cols = slice(r0 * P, r1 * P)
            nc.vector.quantize_mx(
                out=q_codes[:, cols].bitcast(FP8X4),
                scales=q_scales[:, cols],
                in_=q_grouped[:, r0:r1].rearrange("p r s j -> p (r s j)"),
            )

        scores = [keep.tile([P, T], F32, name=f"scores{r}") for r in range(PACK)]
        stages = [keep.tile([P, PACK, CHUNK], F32, name=f"stage{k}", align_bytes=64) for k in range(3)]
        early = keep.tile([P, CHUNK, PACK], BF16, align_bytes=64)
        late = keep.tile([P, M], F32, align_bytes=64)
        w_grouped = [early[:], late[:, M // 2 :].bitcast(BF16).rearrange("p (i r) -> p i r", r=PACK)]
        w_codes = keep.tile([P, I], U32, align_bytes=64)
        w_scales = keep.tile([P, I], U8, align_bytes=64)
        sum_tile = keep.tile([P, 8, CHUNK], F32)
        sums = [[sum_tile[:, 4 * c + e, :] for e in range(4)] for c in range(2)]
        m_grouped = stages[0][:].rearrange("p r i -> p (r i)").bitcast(BF16)
        m_codes = keep.tile([P, E], U32, align_bytes=64)
        m_scales = keep.tile([P, E], U8, align_bytes=64)
        faded = [result[0], result[1], late[:, 0:M], stages[1][:].rearrange("p r i -> p (r i)")]

        def entries(lst, start, count):
            return lst[:, start // 16 : (start + count) // 16]

        def score(r):
            rows = slice(r * P, (r + 1) * P)
            for b in range(T // BANK):
                cols = slice(b * BANK, (b + 1) * BANK)
                bank = banks[(2 * r + b) % 6]
                nc.tensor.matmul_mx(
                    out=bank[:],
                    lhsT=q_codes[:, rows].bitcast(FP8X4),
                    lhsT_scale=q_scales[:, rows],
                    rhs=k_words[:, cols].bitcast(FP8X4),
                    rhs_scale=k_scales[:, cols],
                    start=True,
                    stop=True,
                )
                if b == 0 and r not in (2,):
                    nc.scalar.copy(scores[r][:, cols], bank[:])
                else:
                    nc.vector.tensor_copy(scores[r][:, cols], bank[:])

        def pick(r, c, on_vector=False):
            if on_vector:
                nc.vector.tensor_copy(stages[c][:, r, :], scores[r][:].indirect(entries(list2, c * CHUNK, CHUNK)))
                return
            nc.scalar.activation(stages[c][:, r, :], scores[r][:].indirect(entries(list2, c * CHUNK, CHUNK)), ACT.Copy)

        def differ(r, c):
            nc.vector.tensor_tensor(stages[c + 1][:, r, :], scores[r][:].indirect(entries(list1, c * CHUNK, CHUNK)), stages[c][:, r, :], ALU.subtract)

        def squash(c):
            nc.scalar.activation(stages[(c + 2) % 3][:], stages[c + 1][:], ACT.Sigmoid)

        def quantise_msgs():
            nc.vector.tensor_copy(
                out=m_grouped.rearrange("p (g i j) -> p g j i", i=4, j=PACK),
                in_=m_raw[:].rearrange("p j (g i) -> p g j i", i=4),
            )
            nc.vector.quantize_mx(out=m_codes[:].bitcast(FP8X4), scales=m_scales[:], in_=m_grouped)

        def carry(c):
            nc.vector.tensor_tensor(
                w_grouped[c].rearrange("p (g i) r -> p g r i", i=4),
                stages[(c + 2) % 3][:].rearrange("p r (g i) -> p g r i", i=4),
                qs_cols[:].unsqueeze(1).unsqueeze(3).to_broadcast([P, CHUNK // 4, PACK, 4]),
                ALU.mult,
            )
            cols = slice(c * CHUNK, (c + 1) * CHUNK)
            nc.vector.quantize_mx(
                out=w_codes[:, cols].bitcast(FP8X4),
                scales=w_scales[:, cols],
                in_=w_grouped[c].rearrange("p i r -> p (i r)"),
            )
            for e in ((0, 1, 2, 3), (2, 3, 0, 1))[c]:
                rows = slice(e * P, (e + 1) * P)
                nc.tensor.matmul_mx(
                    out=products(c, e, 1),
                    lhsT=m_codes[:, rows].bitcast(FP8X4),
                    lhsT_scale=m_scales[:, rows],
                    rhs=w_codes[:, cols].bitcast(FP8X4),
                    rhs_scale=w_scales[:, cols],
                    start=True,
                    stop=True,
                )

        def products(c, e, count):
            return banks[2 + 2 * c + e // 2][:, (e % 2) * CHUNK : (e % 2 + count) * CHUNK]

        def pair(c, e):
            first = 4 * c + e
            return sum_tile[:, first : first + 2, :].rearrange("p k i -> p (k i)")

        def scatter(e, c, start, count, on_vector):
            places = windows[e][:].indirect(entries(list3, c * CHUNK + start, count))
            values = sums[c][e][:, start : start + count]
            if on_vector:
                nc.vector.tensor_copy(places, values)
            else:
                nc.scalar.activation(places, values, ACT.Copy)

        def finish(e, pieces):
            for h in range(pieces):
                cols = slice(h * M // pieces, (h + 1) * M // pieces)
                nc.vector.tensor_tensor(result[e][:, cols], faded[e][:, cols], windows[e][:, cols], ALU.add)
                nc.sync.dma_start(out=out[e * P : (e + 1) * P, cols], in_=result[e][:, cols])

        def fading_gpsimd(e, stop):
            nc.gpsimd.tensor_tensor(faded[e][:, 0:stop], result[e][:, 0:stop], fade_wide[:, 0:stop], ALU.mult)

        def fading_vector(e, s0):
            for h in range(2):
                nc.vector.tensor_tensor(by_bank(faded[e], h)[:, s0:, :], by_bank(result[e], h)[:, s0:, :], fade_rows[h][:, s0:, :], ALU.mult)

        fading_gpsimd(0, M)
        for r in range(PACK):
            score(r)
            pick(r, 0)
            if r == PACK - 2:
                differ(0, 0)
        for r in range(1, PACK):
            differ(r, 0)
        squash(0)
        quantise_msgs()
        nc.sync.dma_start(out=result[1], in_=old[P : 2 * P, :])
        carry(0)
        nc.scalar.copy(sums[0][0], products(0, 0, 1))
        for r in range(PACK):
            pick(r, 1, r in ())
            differ(r, 1)
        scatter(0, 0, 0, CHUNK, False)
        squash(1)
        fading_gpsimd(3, 2 * PACK * TAIL)
        carry(1)
        nc.vector.tensor_copy(pair(0, 2), products(0, 2, 2))
        nc.vector.tensor_copy(sums[0][1], products(0, 1, 1))
        fading_vector(1, 0)
        fading_vector(3, TAIL)
        for e in (3, 1, 2):
            scatter(e, 0, 0, CHUNK, False)
        fading_gpsimd(2, M)
        nc.vector.tensor_copy(pair(1, 2), products(1, 2, 2))
        nc.vector.tensor_copy(pair(1, 0), products(1, 0, 2))
        scatter(3, 1, 0, CHUNK, True)
        for e in (2, 0, 1):
            scatter(e, 1, 0, CHUNK, False)
        finish(3, 2)
        finish(2, 2)
        finish(0, 2)
        finish(1, 4)
